import numpy as np, ml_dtypes
CORES = [5,29,101,125,133,157,229,253]
N = 8
TK, NT = 512, 4
def setup_inputs(rng):
    x = rng.standard_normal((NT, 128, TK), dtype=np.float32).astype(ml_dtypes.bfloat16)
    return {"x": np.broadcast_to(x, (2, NT, 128, TK)).reshape(N, 128, TK).copy(), "w": rng.standard_normal((N, 128, NT * 128), dtype=np.float32).astype(ml_dtypes.bfloat16)}
def setup_inputs_big(rng):
    d = setup_inputs(rng)
    for k in ("x", "w"): d[k] = (d[k].astype(np.float32) * 1024.0).astype(d[k].dtype)
    return d
def setup_inputs_small(rng):
    d = setup_inputs(rng)
    for k in ("x", "w"): d[k] = (d[k].astype(np.float32) * (1 / 1024.0)).astype(d[k].dtype)
    return d
def setup_inputs_apart(rng):
    d = setup_inputs(rng)
    f = (10.0 ** rng.permutation(np.linspace(-1.5, 1.5, N))).astype(np.float32).reshape(N, 1, 1)
    for k in ("x", "w"): d[k] = (d[k].astype(np.float32) * f).astype(d[k].dtype)
    return d
def tie_inputs(x):
    x = dict(x)
    x["x"] = np.concatenate([x["x"][:NT], x["x"][:NT]])
    return x
def reference(x, w):
    X, W = x.astype(np.float64), w.astype(np.float64)
    y = np.stack([sum(W[r][:, 128 * j:128 * j + 128].T @ X[j if r < NT else j + NT] for j in range(NT)) for r in range(N)])
    return {"y": y.astype(ml_dtypes.bfloat16 if x.dtype != np.float64 else np.float64)}

@@ -1,0 +1,132 @@
+from concourse.bass import DstId, RemoteDMATransfer
+
+P = 128
+NT = 4
+TK = 512
+HALF = TK // 2
+HOP1_ENGINES = 8
+
+SCRATCH = {
+    "xg": ("sbuf", [P, NT * TK], "bfloat16"),
+    "ws": ("sbuf", [P, NT * P], "bfloat16"),
+    "ys": ("sbuf", [P, TK], "bfloat16"),
+    "half": ("dram", [P, HALF], "bfloat16"),
+    "acc0": ("psum", [P, 512], "float32"),
+    "acc1": ("psum", [P, 512], "float32"),
+}
+SEMAPHORES = (["ld_half", "ld_x", "ld_w", "left", "got", "near"]
+              + ["far%d%d" % (j, s) for j in range(NT) for s in range(2)]
+              + ["mm0", "mm1", "cp0", "cp1", "st0", "st1"])
+
+
+def _engines(mask):
+    return [e for e in range(mask.bit_length()) if (mask >> e) & 1]
+
+
+def _bits(engines):
+    return sum(1 << e for e in engines)
+
+
+def _plan(T, topo):
+    cores = list(T.cores)
+    world = range((max(topo.host(c) for c in cores) + 1) * topo.CORES_PER_HOST)
+    near, far = [], []
+    for r, c in enumerate(cores):
+        s = r // NT
+        others = [d for d in range(len(cores)) if d % NT != r % NT]
+        near += [(r, d) for d in others if topo.may_write(c, cores[d]) and d // NT == s]
+        beyond = [d for d in others if not topo.may_write(c, cores[d])]
+        helpers = [h for h in world
+                   if (topo.host(h), topo.chip(h)) == (topo.host(c), topo.chip(c)) and T.rank_of(h) is None
+                   and all(topo.may_write(h, cores[d]) for d in beyond)]
+        lanes = [[h for h in helpers if topo.die(h) == topo.die(c)], [h for h in helpers if topo.die(h) != topo.die(c)]]
+        for i, d in enumerate(beyond):
+            lane = (i + s) % 2
+            far.append((r, lanes[lane][i // 2], d, lane))
+    return cores, near, far
+
+
+def _table(j):
+    return slice(j * TK, (j + 1) * TK)
+
+
+def _piece(j, s):
+    return slice(j * TK + s * HALF, j * TK + (s + 1) * HALF)
+
+
+def rank_program(g, core, T, topo):
+    cores, near, far = _plan(T, topo)
+    sem = T.sem
+    per_copy = HOP1_ENGINES // NT
+
+    for r, h, d, lane in far:
+        if h == core:
+            rid, pid = topo.addr(cores[d], core)
+            mask = topo.mask(core, cores[d])
+            g.wait_ge(sem.got, per_copy)
+            g.remote_dma(out_ap=T.xg[:, _piece(r % NT, r // NT)], in_ap=T.half[:],
+                         remote_sem=sem["far%d%d" % (r % NT, r // NT)], local_sem=sem.left,
+                         pid=pid, routing_id=rid, dma_engine_mask=mask)
+            g.wait_ge(sem.left, len(_engines(mask)))
+            return
+
+    rank = T.rank_of(core)
+    if rank is None:
+        return
+    j, s = rank % NT, rank // NT
+
+    g.sync.dma_start(T.half[:], T.x[:, s * HALF:(s + 1) * HALF]).then_inc(sem.ld_half, 16)
+    g.sync.dma_start(T.xg[:, _table(j)], T.x[:]).then_inc(sem.ld_x, 16)
+    g.sync.dma_start(T.ws[:], T.w[:]).then_inc(sem.ld_w, 16)
+
+    mine = [e for e in far if e[0] == rank]
+    to_near = [d for r, d in near if r == rank][0]
+    near_mask = topo.mask(core, cores[to_near])
+    on_chip = _engines(min(topo.mask(core, h) for _, h, _, _ in mine))
+    order = [e for e in on_chip if not (near_mask >> e) & 1] + [e for e in on_chip if (near_mask >> e) & 1]
+    use = order[:HOP1_ENGINES]
+    copies = []
+    for t, (_, h, _, _) in enumerate(mine):
+        rid, pid = topo.addr(h, core)
+        copies.append(RemoteDMATransfer(dst_ids=[DstId(rid=rid, pnc=pid)], dma_engine_mask=_bits(use[t::len(mine)]),
+                                        remote_sem=sem.got, src=T.half[:], dst=T.half[:]))
+    g.wait_ge(sem.ld_half, 16)
+    g.remote_dma_fused(copies, local_sem=sem.left)
+    rid, pid = topo.addr(cores[to_near], core)
+    g.wait_ge(sem.ld_x, 16)
+    g.remote_dma(out_ap=T.xg[:, _table(j)], in_ap=T.xg[:, _table(j)], remote_sem=sem.near, local_sem=sem.left,
+                 pid=pid, routing_id=rid, dma_engine_mask=near_mask)
+
+    from_near = [r for r, d in near if d == rank][0]
+    n_near = len(_engines(topo.mask(cores[from_near], core)))
+    landing = [e for e in far if e[2] == rank]
+    halves = sorted(range(2), key=lambda hf: [lane for r, _, _, lane in landing if r // NT == hf][0])
+    acc = [T.acc0, T.acc1]
+
+    def mm(jt, hf, start, stop):
+        return g.tensor.matmul(acc[hf][:, 0:HALF], T.ws[:, jt * P:(jt + 1) * P], T.xg[:, _piece(jt, hf)], start, stop)
+
+    g.tensor.wait_ge(sem.ld_x, 16)
+    g.tensor.wait_ge(sem.ld_w, 16)
+    for hf in halves:
+        mm(j, hf, True, False)
+    g.tensor.wait_ge(sem.near, n_near)
+    for hf in halves:
+        mm(from_near % NT, hf, False, False)
+    for hf in halves:
+        pieces = [e for e in landing if e[0] // NT == hf]
+        for k, (r, h, _, _) in enumerate(pieces):
+            g.tensor.wait_ge(sem["far%d%d" % (r % NT, hf)], len(_engines(topo.mask(h, core))))
+            last = mm(r % NT, hf, False, k == len(pieces) - 1)
+        last.then_inc(sem["mm%d" % hf], 1)
+
+    for hf in halves:
+        g.vector.wait_ge(sem["mm%d" % hf], 1)
+        g.vector.tensor_copy(T.ys[:, hf * HALF:(hf + 1) * HALF], acc[hf][:, 0:HALF]).then_inc(sem["cp%d" % hf], 1)
+
+    for q, hf in zip((g.sync, g.scalar), halves):
+        q.wait_ge(sem["cp%d" % hf], 1)
+        q.dma_start(T.y[:, hf * HALF:(hf + 1) * HALF], T.ys[:, hf * HALF:(hf + 1) * HALF]).then_inc(sem["st%d" % hf], 16)
+        q.wait_ge(sem["st%d" % hf], 16)
+
+    g.wait_ge(sem.left, HOP1_ENGINES + len(_engines(near_mask)))

@@ -4,6 +4,7 @@ P = 128
 NT = 4
 TK = 512
 HALF = TK // 2
+QW = HALF // 2
 HOP1_ENGINES = 8
 
 SCRATCH = {
@@ -13,10 +14,12 @@ SCRATCH = {
     "half": ("dram", [P, HALF], "bfloat16"),
     "acc0": ("psum", [P, 512], "float32"),
     "acc1": ("psum", [P, 512], "float32"),
+    "acc2": ("psum", [P, 512], "float32"),
+    "acc3": ("psum", [P, 512], "float32"),
 }
 SEMAPHORES = (["ld_half", "ld_x", "ld_w", "left", "got", "near"]
               + ["far%d%d" % (j, s) for j in range(NT) for s in range(2)]
-              + ["mm0", "mm1", "cp0", "cp1", "st0", "st1"])
+              + ["mm0", "mm1", "mm2", "mm3", "cp0", "cp1", "st0", "st1"])
 
 
 def _engines(mask):
@@ -36,13 +39,15 @@ def _plan(T, topo):
         others = [d for d in range(len(cores)) if d % NT != r % NT]
         near += [(r, d) for d in others if topo.may_write(c, cores[d]) and d // NT == s]
         beyond = [d for d in others if not topo.may_write(c, cores[d])]
+        jj = sorted({d % NT for d in range(len(cores)) if d not in beyond}).index(r % NT)
         helpers = [h for h in world
                    if (topo.host(h), topo.chip(h)) == (topo.host(c), topo.chip(c)) and T.rank_of(h) is None
                    and all(topo.may_write(h, cores[d]) for d in beyond)]
         lanes = [[h for h in helpers if topo.die(h) == topo.die(c)], [h for h in helpers if topo.die(h) != topo.die(c)]]
         for i, d in enumerate(beyond):
-            lane = (i + s) % 2
-            far.append((r, lanes[lane][i // 2], d, lane))
+            step = (s + i) % 2
+            lane = (jj + i // 2) % 2
+            far.append((r, lanes[lane][step], d, lane, step))
     return cores, near, far
 
 
@@ -57,13 +62,13 @@ def _piece(j, s):
 def rank_program(g, core, T, topo):
     cores, near, far = _plan(T, topo)
     sem = T.sem
-    per_copy = HOP1_ENGINES // NT
+    per_lane = HOP1_ENGINES // 2
 
-    for r, h, d, lane in far:
+    for r, h, d, lane, step in far:
         if h == core:
             rid, pid = topo.addr(cores[d], core)
             mask = topo.mask(core, cores[d])
-            g.wait_ge(sem.got, per_copy)
+            g.wait_ge(sem.got, per_lane)
             g.remote_dma(out_ap=T.xg[:, _piece(r % NT, r // NT)], in_ap=T.half[:],
                          remote_sem=sem["far%d%d" % (r % NT, r // NT)], local_sem=sem.left,
                          pid=pid, routing_id=rid, dma_engine_mask=mask)
@@ -82,14 +87,16 @@ def rank_program(g, core, T, topo):
     mine = [e for e in far if e[0] == rank]
     to_near = [d for r, d in near if r == rank][0]
     near_mask = topo.mask(core, cores[to_near])
-    on_chip = _engines(min(topo.mask(core, h) for _, h, _, _ in mine))
+    on_chip = _engines(min(topo.mask(core, e[1]) for e in mine))
     order = [e for e in on_chip if not (near_mask >> e) & 1] + [e for e in on_chip if (near_mask >> e) & 1]
     use = order[:HOP1_ENGINES]
     copies = []
-    for t, (_, h, _, _) in enumerate(mine):
-        rid, pid = topo.addr(h, core)
-        copies.append(RemoteDMATransfer(dst_ids=[DstId(rid=rid, pnc=pid)], dma_engine_mask=_bits(use[t::len(mine)]),
-                                        remote_sem=sem.got, src=T.half[:], dst=T.half[:]))
+    for lane in range(2):
+        hs = [e[1] for e in sorted((e for e in mine if e[3] == lane), key=lambda e: e[4])]
+        ids = [topo.addr(h, core) for h in hs]
+        copies.append(RemoteDMATransfer(dst_ids=[DstId(rid=rid, pnc=pid) for rid, pid in ids],
+                                        dma_engine_mask=_bits(use[lane::2]), remote_sem=sem.got,
+                                        srcs=[T.half[:]], dsts=[T.half[:] for _ in hs]))
     g.wait_ge(sem.ld_half, 16)
     g.remote_dma_fused(copies, local_sem=sem.left)
     rid, pid = topo.addr(cores[to_near], core)
@@ -100,32 +107,37 @@ def rank_program(g, core, T, topo):
     from_near = [r for r, d in near if d == rank][0]
     n_near = len(_engines(topo.mask(cores[from_near], core)))
     landing = [e for e in far if e[2] == rank]
-    halves = sorted(range(2), key=lambda hf: [lane for r, _, _, lane in landing if r // NT == hf][0])
-    acc = [T.acc0, T.acc1]
+    halves = sorted(range(2), key=lambda hf: [e[4] for e in landing if e[0] // NT == hf][0])
+    quarters = [(hf, k) for hf in halves for k in range(2)]
 
-    def mm(jt, hf, start, stop):
-        return g.tensor.matmul(acc[hf][:, 0:HALF], T.ws[:, jt * P:(jt + 1) * P], T.xg[:, _piece(jt, hf)], start, stop)
+    def mm(jt, hf, k, start, stop):
+        lo = jt * TK + hf * HALF + k * QW
+        return g.tensor.matmul(T["acc%d" % (2 * hf + k)][:, 0:QW], T.ws[:, jt * P:(jt + 1) * P], T.xg[:, lo:lo + QW],
+                               start, stop)
 
     g.tensor.wait_ge(sem.ld_x, 16)
     g.tensor.wait_ge(sem.ld_w, 16)
-    for hf in halves:
-        mm(j, hf, True, False)
+    for hf, k in quarters:
+        mm(j, hf, k, True, False)
     g.tensor.wait_ge(sem.near, n_near)
+    for hf, k in quarters:
+        mm(from_near % NT, hf, k, False, False)
     for hf in halves:
-        mm(from_near % NT, hf, False, False)
-    for hf in halves:
-        pieces = [e for e in landing if e[0] // NT == hf]
-        for k, (r, h, _, _) in enumerate(pieces):
-            g.tensor.wait_ge(sem["far%d%d" % (r % NT, hf)], len(_engines(topo.mask(h, core))))
-            last = mm(r % NT, hf, False, k == len(pieces) - 1)
-        last.then_inc(sem["mm%d" % hf], 1)
+        first, second = sorted((e for e in landing if e[0] // NT == hf), key=lambda e: e[3])
+        g.tensor.wait_ge(sem["far%d%d" % (first[0] % NT, hf)], len(_engines(topo.mask(first[1], core))))
+        for k in range(2):
+            mm(first[0] % NT, hf, k, False, False)
+        g.tensor.wait_ge(sem["far%d%d" % (second[0] % NT, hf)], len(_engines(topo.mask(second[1], core))))
+        for k in range(2):
+            mm(second[0] % NT, hf, k, False, True).then_inc(sem["mm%d" % (2 * hf + k)], 1)
 
-    for hf in halves:
-        g.vector.wait_ge(sem["mm%d" % hf], 1)
-        g.vector.tensor_copy(T.ys[:, hf * HALF:(hf + 1) * HALF], acc[hf][:, 0:HALF]).then_inc(sem["cp%d" % hf], 1)
+    for hf, k in quarters:
+        lo = hf * HALF + k * QW
+        g.vector.wait_ge(sem["mm%d" % (2 * hf + k)], 1)
+        g.vector.tensor_copy(T.ys[:, lo:lo + QW], T["acc%d" % (2 * hf + k)][:, 0:QW]).then_inc(sem["cp%d" % hf], 1)
 
     for q, hf in zip((g.sync, g.scalar), halves):
-        q.wait_ge(sem["cp%d" % hf], 1)
+        q.wait_ge(sem["cp%d" % hf], 2)
         q.dma_start(T.y[:, hf * HALF:(hf + 1) * HALF], T.ys[:, hf * HALF:(hf + 1) * HALF]).then_inc(sem["st%d" % hf], 16)
         q.wait_ge(sem["st%d" % hf], 16)
 

@@ -5,19 +5,21 @@ NT = 4
 TK = 512
 HALF = TK // 2
 QW = HALF // 2
+HW = 8
 HOP1_ENGINES = 8
 
 SCRATCH = {
     "xg": ("sbuf", [P, NT * TK], "bfloat16"),
     "ws": ("sbuf", [P, NT * P], "bfloat16"),
     "ys": ("sbuf", [P, TK], "bfloat16"),
-    "half": ("dram", [P, HALF], "bfloat16"),
+    "head": ("dram", [P, HW], "bfloat16"),
+    "body": ("dram", [P, HALF - HW], "bfloat16"),
     "acc0": ("psum", [P, 512], "float32"),
     "acc1": ("psum", [P, 512], "float32"),
     "acc2": ("psum", [P, 512], "float32"),
     "acc3": ("psum", [P, 512], "float32"),
 }
-SEMAPHORES = (["ld_half", "ld_x", "ld_w", "left", "got", "near"]
+SEMAPHORES = (["ld_head", "ld_body", "ld_x", "ld_w", "left", "got_head", "got", "near"]
               + ["far%d%d" % (j, s) for j in range(NT) for s in range(2)]
               + ["mm0", "mm1", "mm2", "mm3", "cp0", "cp1", "st0", "st1"])
 
@@ -55,8 +57,12 @@ def _table(j):
     return slice(j * TK, (j + 1) * TK)
 
 
-def _piece(j, s):
-    return slice(j * TK + s * HALF, j * TK + (s + 1) * HALF)
+def _head(j, s):
+    return slice(j * TK + s * HALF, j * TK + s * HALF + HW)
+
+
+def _body(j, s):
+    return slice(j * TK + s * HALF + HW, j * TK + (s + 1) * HALF)
 
 
 def rank_program(g, core, T, topo):
@@ -68,11 +74,14 @@ def rank_program(g, core, T, topo):
         if h == core:
             rid, pid = topo.addr(cores[d], core)
             mask = topo.mask(core, cores[d])
+            arrived = sem["far%d%d" % (r % NT, r // NT)]
+            g.wait_ge(sem.got_head, 1)
+            g.remote_dma(out_ap=T.xg[:, _head(r % NT, r // NT)], in_ap=T.head[:], remote_sem=arrived,
+                         local_sem=sem.left, pid=pid, routing_id=rid, dma_engine_mask=mask)
             g.wait_ge(sem.got, per_lane)
-            g.remote_dma(out_ap=T.xg[:, _piece(r % NT, r // NT)], in_ap=T.half[:],
-                         remote_sem=sem["far%d%d" % (r % NT, r // NT)], local_sem=sem.left,
-                         pid=pid, routing_id=rid, dma_engine_mask=mask)
-            g.wait_ge(sem.left, len(_engines(mask)))
+            g.remote_dma(out_ap=T.xg[:, _body(r % NT, r // NT)], in_ap=T.body[:], remote_sem=arrived,
+                         local_sem=sem.left, pid=pid, routing_id=rid, dma_engine_mask=mask)
+            g.wait_ge(sem.left, 2 * len(_engines(mask)))
             return
 
     rank = T.rank_of(core)
@@ -80,9 +89,10 @@ def rank_program(g, core, T, topo):
         return
     j, s = rank % NT, rank // NT
 
-    g.sync.dma_start(T.half[:], T.x[:, s * HALF:(s + 1) * HALF]).then_inc(sem.ld_half, 16)
+    g.sync.dma_start(T.head[:], T.x[:, s * HALF:s * HALF + HW]).then_inc(sem.ld_head, 16)
+    g.scalar.dma_start(T.body[:], T.x[:, s * HALF + HW:(s + 1) * HALF]).then_inc(sem.ld_body, 16)
     g.sync.dma_start(T.xg[:, _table(j)], T.x[:]).then_inc(sem.ld_x, 16)
-    g.sync.dma_start(T.ws[:], T.w[:]).then_inc(sem.ld_w, 16)
+    g.scalar.dma_start(T.ws[:], T.w[:]).then_inc(sem.ld_w, 16)
 
     mine = [e for e in far if e[0] == rank]
     to_near = [d for r, d in near if r == rank][0]
@@ -90,19 +100,22 @@ def rank_program(g, core, T, topo):
     on_chip = _engines(min(topo.mask(core, e[1]) for e in mine))
     order = [e for e in on_chip if not (near_mask >> e) & 1] + [e for e in on_chip if (near_mask >> e) & 1]
     use = order[:HOP1_ENGINES]
-    copies = []
+    heads, copies = [], []
     for lane in range(2):
         hs = [e[1] for e in sorted((e for e in mine if e[3] == lane), key=lambda e: e[4])]
-        ids = [topo.addr(h, core) for h in hs]
-        copies.append(RemoteDMATransfer(dst_ids=[DstId(rid=rid, pnc=pid) for rid, pid in ids],
-                                        dma_engine_mask=_bits(use[lane::2]), remote_sem=sem.got,
-                                        srcs=[T.half[:]], dsts=[T.half[:] for _ in hs]))
-    g.wait_ge(sem.ld_half, 16)
-    g.remote_dma_fused(copies, local_sem=sem.left)
+        ids = [DstId(rid=rid, pnc=pid) for rid, pid in (topo.addr(h, core) for h in hs)]
+        heads.append(RemoteDMATransfer(dst_ids=ids, dma_engine_mask=_bits(use[lane::2][:1]), remote_sem=sem.got_head,
+                                       srcs=[T.head[:]], dsts=[T.head[:] for _ in hs]))
+        copies.append(RemoteDMATransfer(dst_ids=ids, dma_engine_mask=_bits(use[lane::2]), remote_sem=sem.got,
+                                        srcs=[T.body[:]], dsts=[T.body[:] for _ in hs]))
+    g.wait_ge(sem.ld_head, 16)
+    g.remote_dma_fused(heads, local_sem=sem.left)
     rid, pid = topo.addr(cores[to_near], core)
     g.wait_ge(sem.ld_x, 16)
     g.remote_dma(out_ap=T.xg[:, _table(j)], in_ap=T.xg[:, _table(j)], remote_sem=sem.near, local_sem=sem.left,
                  pid=pid, routing_id=rid, dma_engine_mask=near_mask)
+    g.wait_ge(sem.ld_body, 16)
+    g.remote_dma_fused(copies, local_sem=sem.left)
 
     from_near = [r for r, d in near if d == rank][0]
     n_near = len(_engines(topo.mask(cores[from_near], core)))
@@ -124,10 +137,10 @@ def rank_program(g, core, T, topo):
         mm(from_near % NT, hf, k, False, False)
     for hf in halves:
         first, second = sorted((e for e in landing if e[0] // NT == hf), key=lambda e: e[3])
-        g.tensor.wait_ge(sem["far%d%d" % (first[0] % NT, hf)], len(_engines(topo.mask(first[1], core))))
+        g.tensor.wait_ge(sem["far%d%d" % (first[0] % NT, hf)], 2 * len(_engines(topo.mask(first[1], core))))
         for k in range(2):
             mm(first[0] % NT, hf, k, False, False)
-        g.tensor.wait_ge(sem["far%d%d" % (second[0] % NT, hf)], len(_engines(topo.mask(second[1], core))))
+        g.tensor.wait_ge(sem["far%d%d" % (second[0] % NT, hf)], 2 * len(_engines(topo.mask(second[1], core))))
         for k in range(2):
             mm(second[0] % NT, hf, k, False, True).then_inc(sem["mm%d" % (2 * hf + k)], 1)
 
@@ -141,4 +154,4 @@ def rank_program(g, core, T, topo):
         q.dma_start(T.y[:, hf * HALF:(hf + 1) * HALF], T.ys[:, hf * HALF:(hf + 1) * HALF]).then_inc(sem["st%d" % hf], 16)
         q.wait_ge(sem["st%d" % hf], 16)
 
-    g.wait_ge(sem.left, HOP1_ENGINES + len(_engines(near_mask)))
+    g.wait_ge(sem.left, len(heads) + HOP1_ENGINES + len(_engines(near_mask)))

from concourse.bass import DstId, RemoteDMATransfer

P = 128
NT = 4
TK = 512
HALF = TK // 2
QW = HALF // 2
HW = 8
HOP1_ENGINES = 8

SCRATCH = {
    "xg": ("sbuf", [P, NT * TK], "bfloat16"),
    "ws": ("sbuf", [P, NT * P], "bfloat16"),
    "ys": ("sbuf", [P, TK], "bfloat16"),
    "head": ("dram", [P, HW], "bfloat16"),
    "body": ("dram", [P, HALF - HW], "bfloat16"),
    "acc0": ("psum", [P, 512], "float32"),
    "acc1": ("psum", [P, 512], "float32"),
    "acc2": ("psum", [P, 512], "float32"),
    "acc3": ("psum", [P, 512], "float32"),
}
SEMAPHORES = (["ld_head", "ld_body", "ld_x", "ld_w", "left", "got_head", "got", "near"]
              + ["far%d%d" % (j, s) for j in range(NT) for s in range(2)]
              + ["mm0", "mm1", "mm2", "mm3", "cp0", "cp1", "st0", "st1"])


def _engines(mask):
    return [e for e in range(mask.bit_length()) if (mask >> e) & 1]


def _bits(engines):
    return sum(1 << e for e in engines)


def _plan(T, topo):
    cores = list(T.cores)
    world = range((max(topo.host(c) for c in cores) + 1) * topo.CORES_PER_HOST)
    near, far = [], []
    for r, c in enumerate(cores):
        s = r // NT
        others = [d for d in range(len(cores)) if d % NT != r % NT]
        near += [(r, d) for d in others if topo.may_write(c, cores[d]) and d // NT == s]
        beyond = [d for d in others if not topo.may_write(c, cores[d])]
        jj = sorted({d % NT for d in range(len(cores)) if d not in beyond}).index(r % NT)
        helpers = [h for h in world
                   if (topo.host(h), topo.chip(h)) == (topo.host(c), topo.chip(c)) and T.rank_of(h) is None
                   and all(topo.may_write(h, cores[d]) for d in beyond)]
        lanes = [[h for h in helpers if topo.die(h) == topo.die(c)], [h for h in helpers if topo.die(h) != topo.die(c)]]
        for i, d in enumerate(beyond):
            step = (s + i) % 2
            lane = (jj + i // 2) % 2
            far.append((r, lanes[lane][step], d, lane, step))
    return cores, near, far


def _table(j):
    return slice(j * TK, (j + 1) * TK)


def _head(j, s):
    return slice(j * TK + s * HALF, j * TK + s * HALF + HW)


def _body(j, s):
    return slice(j * TK + s * HALF + HW, j * TK + (s + 1) * HALF)


def rank_program(g, core, T, topo):
    cores, near, far = _plan(T, topo)
    sem = T.sem
    per_lane = HOP1_ENGINES // 2

    for r, h, d, lane, step in far:
        if h == core:
            rid, pid = topo.addr(cores[d], core)
            mask = topo.mask(core, cores[d])
            arrived = sem["far%d%d" % (r % NT, r // NT)]
            g.wait_ge(sem.got_head, 1)
            g.remote_dma(out_ap=T.xg[:, _head(r % NT, r // NT)], in_ap=T.head[:], remote_sem=arrived,
                         local_sem=sem.left, pid=pid, routing_id=rid, dma_engine_mask=mask)
            g.wait_ge(sem.got, per_lane)
            g.remote_dma(out_ap=T.xg[:, _body(r % NT, r // NT)], in_ap=T.body[:], remote_sem=arrived,
                         local_sem=sem.left, pid=pid, routing_id=rid, dma_engine_mask=mask)
            g.wait_ge(sem.left, 2 * len(_engines(mask)))
            return

    rank = T.rank_of(core)
    if rank is None:
        return
    j, s = rank % NT, rank // NT

    g.sync.dma_start(T.head[:], T.x[:, s * HALF:s * HALF + HW]).then_inc(sem.ld_head, 16)
    g.scalar.dma_start(T.body[:], T.x[:, s * HALF + HW:(s + 1) * HALF]).then_inc(sem.ld_body, 16)
    g.sync.dma_start(T.xg[:, _table(j)], T.x[:]).then_inc(sem.ld_x, 16)
    g.scalar.dma_start(T.ws[:], T.w[:]).then_inc(sem.ld_w, 16)

    mine = [e for e in far if e[0] == rank]
    to_near = [d for r, d in near if r == rank][0]
    near_mask = topo.mask(core, cores[to_near])
    on_chip = _engines(min(topo.mask(core, e[1]) for e in mine))
    order = [e for e in on_chip if not (near_mask >> e) & 1] + [e for e in on_chip if (near_mask >> e) & 1]
    use = order[:HOP1_ENGINES]
    heads, copies = [], []
    for lane in range(2):
        hs = [e[1] for e in sorted((e for e in mine if e[3] == lane), key=lambda e: e[4])]
        ids = [DstId(rid=rid, pnc=pid) for rid, pid in (topo.addr(h, core) for h in hs)]
        heads.append(RemoteDMATransfer(dst_ids=ids, dma_engine_mask=_bits(use[lane::2][:1]), remote_sem=sem.got_head,
                                       srcs=[T.head[:]], dsts=[T.head[:] for _ in hs]))
        copies.append(RemoteDMATransfer(dst_ids=ids, dma_engine_mask=_bits(use[lane::2]), remote_sem=sem.got,
                                        srcs=[T.body[:]], dsts=[T.body[:] for _ in hs]))
    g.wait_ge(sem.ld_head, 16)
    g.remote_dma_fused(heads, local_sem=sem.left)
    rid, pid = topo.addr(cores[to_near], core)
    g.wait_ge(sem.ld_x, 16)
    g.remote_dma(out_ap=T.xg[:, _table(j)], in_ap=T.xg[:, _table(j)], remote_sem=sem.near, local_sem=sem.left,
                 pid=pid, routing_id=rid, dma_engine_mask=near_mask)
    g.wait_ge(sem.ld_body, 16)
    g.remote_dma_fused(copies, local_sem=sem.left)

    from_near = [r for r, d in near if d == rank][0]
    n_near = len(_engines(topo.mask(cores[from_near], core)))
    landing = [e for e in far if e[2] == rank]
    halves = sorted(range(2), key=lambda hf: [e[4] for e in landing if e[0] // NT == hf][0])
    quarters = [(hf, k) for hf in halves for k in range(2)]

    def mm(jt, hf, k, start, stop):
        lo = jt * TK + hf * HALF + k * QW
        return g.tensor.matmul(T["acc%d" % (2 * hf + k)][:, 0:QW], T.ws[:, jt * P:(jt + 1) * P], T.xg[:, lo:lo + QW],
                               start, stop)

    g.tensor.wait_ge(sem.ld_x, 16)
    g.tensor.wait_ge(sem.ld_w, 16)
    for hf, k in quarters:
        mm(j, hf, k, True, False)
    g.tensor.wait_ge(sem.near, n_near)
    for hf, k in quarters:
        mm(from_near % NT, hf, k, False, False)
    for hf in halves:
        first, second = sorted((e for e in landing if e[0] // NT == hf), key=lambda e: e[3])
        g.tensor.wait_ge(sem["far%d%d" % (first[0] % NT, hf)], 2 * len(_engines(topo.mask(first[1], core))))
        for k in range(2):
            mm(first[0] % NT, hf, k, False, False)
        g.tensor.wait_ge(sem["far%d%d" % (second[0] % NT, hf)], 2 * len(_engines(topo.mask(second[1], core))))
        for k in range(2):
            mm(second[0] % NT, hf, k, False, True).then_inc(sem["mm%d" % (2 * hf + k)], 1)

    for hf, k in quarters:
        lo = hf * HALF + k * QW
        g.vector.wait_ge(sem["mm%d" % (2 * hf + k)], 1)
        g.vector.tensor_copy(T.ys[:, lo:lo + QW], T["acc%d" % (2 * hf + k)][:, 0:QW]).then_inc(sem["cp%d" % hf], 1)

    for q, hf in zip((g.sync, g.scalar), halves):
        q.wait_ge(sem["cp%d" % hf], 2)
        q.dma_start(T.y[:, hf * HALF:(hf + 1) * HALF], T.ys[:, hf * HALF:(hf + 1) * HALF]).then_inc(sem["st%d" % hf], 16)
        q.wait_ge(sem["st%d" % hf], 16)

    g.wait_ge(sem.left, len(heads) + HOP1_ENGINES + len(_engines(near_mask)))
